import numpy as np
import ml_dtypes


def mxq(x, axis, fmt="e4m3"):
    dtype, down = {"e4m3": (ml_dtypes.float8_e4m3fn, 7), "e5m2": (ml_dtypes.float8_e5m2, 14)}[fmt]
    v = np.moveaxis(np.asarray(x, np.float32).astype(ml_dtypes.bfloat16).astype(np.float64), axis, -1)
    blocks = v.reshape(v.shape[:-1] + (-1, 32))
    amax = np.abs(blocks).max(-1, keepdims=True)
    byte = np.maximum(np.where(amax > 0, np.frexp(amax)[1] - 1 + 127, 0) - down, 1)
    scale = np.exp2(byte - 127.0)
    codes = (blocks / scale).astype(np.float32).astype(dtype).astype(np.float64)
    return np.moveaxis((codes * scale).reshape(v.shape), -1, axis)


WIDE = False


def mx_kscale(k):
    if not WIDE:
        return np.ones(k)
    levels = np.array([10, -10, 5, -5, 0])
    if k % 512:
        return np.exp2(np.random.permutation(np.resize(levels, k // 32))).repeat(32)
    a = np.empty((k // 512, 16))
    for p in range(k // 512):
        a[p, :8] = np.random.permutation(np.resize(levels, 8))
        for g in range(8):
            far = levels[np.abs(levels - a[p, g]) >= 10]
            a[p, g + 8] = far[np.random.randint(len(far))]
    return np.exp2(a.ravel()).repeat(32)


def f64(x):
    return np.asarray(x).astype(np.float64)


def striped(idx):
    return np.tile(idx.reshape(-1, 16).T, (8, 1)).astype(np.uint16)


def unstriped(offs):
    return offs[:16].T.reshape(-1).astype(np.int64)


def striped8(idx):
    return np.concatenate([x.reshape(-1, 16).T for x in idx]).astype(np.uint16)


def runs(offs, k):
    lists = np.stack([offs[16 * r : 16 * r + 16].T.reshape(-1) for r in range(8)]).astype(np.int64)
    return lists[np.arange(k) % 512 // 64]


def pack_weight(w):
    k, n = w.shape
    w = f64(np.asarray(w, np.float32).astype(ml_dtypes.bfloat16)).reshape(k // 32, 32, n)
    amax = np.abs(w).max(1)
    byte = np.clip(np.where(amax > 0, np.frexp(amax)[1] - 1 + 127 - 7, 1), 1, 254)
    scaled = (w * np.exp2(127.0 - byte)[:, None, :]).reshape(k, n).astype(np.float32)
    words = np.ascontiguousarray(scaled.reshape(k // 512, 128, 4, n).transpose(0, 1, 3, 2)).astype(ml_dtypes.float8_e4m3fn).view(np.uint8)
    return words, np.ascontiguousarray(byte.astype(np.uint8).reshape(k // 512, 16, n))


def unpack_weight(words, scales):
    g, p, n, _ = words.shape
    vals = np.ascontiguousarray(words).view(ml_dtypes.float8_e4m3fn).astype(np.float64) * np.repeat(np.exp2(scales.astype(np.float64) - 127.0), 8, axis=1)[..., None]
    return vals.transpose(0, 1, 3, 2).reshape(g * 512, n)

def planes(y):
    n, m = y.shape
    v = y.astype(np.float32).astype(ml_dtypes.bfloat16).astype(np.float64).reshape(n // 32, 32, m)
    top = np.abs(v).max(1)
    byte = np.clip(np.where(top > 0, np.frexp(top)[1] - 1 + 127 - 7, 1), 1, 254)
    codes = (v * np.exp2(127.0 - byte)[:, None, :]).reshape(n, m).astype(np.float32).astype(ml_dtypes.float8_e4m3fn).view(np.uint8)
    words = codes.reshape(n // 512, 128, 4, m).transpose(0, 1, 3, 2)
    return np.ascontiguousarray(words), np.ascontiguousarray(byte.astype(np.uint8).reshape(n // 512, 16, m))


K, T, S, H = 512, 2048, 512, 512


def setup_inputs():
    n = np.random.standard_normal
    s = mx_kscale(K)[:, None]
    u = mx_kscale(S)
    packed_xT = pack_weight(n((K, T)) * s)
    packed_w1 = pack_weight(n((K, H)) / np.sqrt(K) / s)
    return {
        "x_words": packed_xT[0],
        "x_scales": packed_xT[1],
        "w1_words": packed_w1[0],
        "w1_scales": packed_w1[1],
        "ga": (np.random.uniform(0.5, 1.5, (H, 1)) * u[:, None]).astype(np.float32),
        "gb": (np.random.uniform(0.5, 1.5, (H, 1)) / u[:, None]).astype(np.float32),
        "offs": striped(np.random.permutation(T)[:S]),
        "n1": striped8(np.stack([np.random.permutation(S) for _ in range(8)])),
        "n2": striped8(np.stack([np.random.permutation(S) for _ in range(8)])),
        "cq": striped8(np.stack([np.random.permutation(S) for _ in range(8)])),
    }


def reference(x_words, x_scales, w1_words, w1_scales, ga, gb, offs, n1, n2, cq):
    xq = unpack_weight(x_words, x_scales)[:, unstriped(offs)]
    y = unpack_weight(w1_words, w1_scales).T @ xq
    z = f64(ga) * (y[np.arange(H)[:, None], runs(n1, H)])
    z2 = f64(gb) * (y - (y[np.arange(H)[:, None], runs(n2, H)]))
    s = 0.0625 * ((mxq(z, 0, "e4m3").T @ mxq(z2, 0, "e4m3")))
    out_0 = np.tanh(s + s[np.arange(S)[:, None], runs(cq, S)])
    return (out_0,) + planes(out_0)

@@ -1,0 +1,216 @@
+from contextlib import ExitStack
+
+import concourse.mybir as mybir
+
+F32 = mybir.dt.float32
+BF16 = mybir.dt.bfloat16
+I32 = mybir.dt.int32
+U32 = mybir.dt.uint32
+U16 = mybir.dt.uint16
+U8 = mybir.dt.uint8
+FP8X4 = mybir.dt.float8_e4m3fn_x4
+ALU = mybir.AluOpType
+ACT = mybir.ActivationFunctionType
+
+P = 128
+PACK = 4
+T = 2048
+S = 512
+HALF = S // 2
+FLOPS = 2 * 2 * 512 * 512 * 512
+
+
+def tile_picked_autoc8_none_po_kernel(
+    tc, x_words, x_scales, w1_words, w1_scales, ga, gb, offs, n1, n2, cq, out_0, out_1, out_2
+):
+    nc = tc.nc
+
+    def entries(list_tile, j0, j1):
+        return list_tile[:, j0 // 16 : j1 // 16]
+
+    def halfcols(h):
+        return slice(h * HALF, (h + 1) * HALF)
+
+    with ExitStack() as ctx:
+        lists = ctx.enter_context(tc.tile_pool(name="lists", bufs=1))
+        keep = ctx.enter_context(tc.tile_pool(name="keep", bufs=1))
+        psum = ctx.enter_context(tc.psum_pool(name="psum", bufs=8))
+
+        offs_t = lists.tile([P, S // 16], U16, name="offs_t")
+        n1_t = lists.tile([P, S // 16], U16, name="n1_t")
+        n2_t = lists.tile([P, S // 16], U16, name="n2_t")
+        cq_t = lists.tile([P, S // 16], U16, name="cq_t")
+
+        x_w = keep.tile([P, T], U32, name="x_w", align_bytes=64)
+        x_s = keep.tile([P, T], U8, name="x_s", align_bytes=64)
+        w_w = keep.tile([P, S], U32, name="w_w", align_bytes=64)
+        w_s = keep.tile([P, S], U8, name="w_s", align_bytes=64)
+        ga_t = keep.tile([P, PACK], F32, name="ga_t")
+        gb_t = keep.tile([P, PACK], F32, name="gb_t")
+        ngb_t = keep.tile([P, PACK], F32, name="ngb_t")
+        warm_out = keep.tile([P, 1], F32, name="warm_out")
+
+        nc.vector.memset(x_s[:].bitcast(I32), 0)
+        nc.gpsimd.memset(w_s[:].bitcast(I32), 0)
+
+        def load_scale_rows(queue, plane, scales, q):
+            queue.dma_start(plane[32 * q : 32 * q + 4, :].bitcast(I32), scales[0, 4 * q : 4 * q + 4, :].bitcast(I32))
+
+        nc.sync.dma_start(offs_t[:], offs)
+        nc.sync.dma_start(n1_t[:], n1)
+        nc.sync.dma_start(n2_t[:], n2)
+        nc.sync.dma_start(cq_t[:], cq)
+        nc.sync.dma_start(w_w[:].bitcast(I32), w1_words[0].rearrange("p n t -> p (n t)").bitcast(I32))
+        nc.sync.dma_start(x_w[:].bitcast(I32), x_words[0].rearrange("p n t -> p (n t)").bitcast(I32))
+        for q in range(4):
+            load_scale_rows(nc.scalar, x_s, x_scales, q)
+        for q in range(2):
+            load_scale_rows(nc.scalar, w_s, w1_scales, q)
+        nc.gpsimd.dma_start(ga_t[:], ga.rearrange("(p t) o -> p (t o)", t=PACK))
+        for q in range(2, 4):
+            load_scale_rows(nc.gpsimd, w_s, w1_scales, q)
+        nc.gpsimd.dma_start(gb_t[:], gb.rearrange("(p t) o -> p (t o)", t=PACK))
+        nc.scalar.activation(out=warm_out[:], in_=ga_t[:, 0:1], func=ACT.Tanh)
+
+        nc.gpsimd.tensor_scalar(out=ngb_t[:], in0=gb_t[:], scalar1=-1.0, scalar2=0.0, op0=ALU.mult, op1=ALU.add)
+
+        wd_w = keep.tile([P, S], U32, name="wd_w", align_bytes=64)
+        wd_s = keep.tile([P, S], U8, name="wd_s", align_bytes=64)
+        nc.vector.tensor_copy(
+            out=wd_w[:].rearrange("p (t a i) -> p a t i", t=PACK, i=4),
+            in_=w_w[:].rearrange("p (a i t) -> p a t i", t=PACK, i=4),
+        )
+        xg_s = keep.tile([P, S], U8, name="xg_s", align_bytes=64)
+        nc.vector.tensor_copy(out=xg_s[:], in_=x_s[:].indirect(offs_t[:]))
+        nc.vector.tensor_copy(
+            out=wd_s[:].rearrange("p (t a i) -> p a t i", t=PACK, i=16),
+            in_=w_s[:].rearrange("p (a i t) -> p a t i", t=PACK, i=16),
+        )
+        xg_w = keep.tile([P, S], U32, name="xg_w", align_bytes=64)
+        for h in range(2):
+            nc.vector.tensor_copy(out=xg_w[:, halfcols(h)], in_=x_w[:].indirect(entries(offs_t, h * HALF, (h + 1) * HALF)))
+
+        a_win = [keep.tile([P, S], F32, name="a_win%d" % t) for t in range(PACK)]
+        n_win = [keep.tile([P, S], F32, name="n_win%d" % t) for t in range(PACK)]
+        n_cpy = [keep.tile([P, S], F32, name="n_cpy%d" % t) for t in range(PACK)]
+        for t in range(PACK):
+            rows = slice(t * P, (t + 1) * P)
+            pieces = [halfcols(0), halfcols(1)] if t == 0 else [slice(0, S)]
+            banks = []
+            for cols in pieces:
+                bank = psum.tile([P, cols.stop - cols.start], F32, name="bank", tag="bank")
+                nc.tensor.matmul_mx(
+                    out=bank[:], lhsT=wd_w[:, rows].bitcast(FP8X4), lhsT_scale=wd_s[:, rows],
+                    rhs=xg_w[:, cols].bitcast(FP8X4), rhs_scale=xg_s[:, cols], start=True, stop=True,
+                )
+                banks.append(bank)
+            for cols, bank in zip(pieces, banks):
+                nc.scalar.activation(out=a_win[t][:, cols], in_=bank[:], func=ACT.Copy, scale=ga_t[:, t : t + 1])
+            for cols, bank in zip(pieces, banks):
+                nc.scalar.activation(out=n_win[t][:, cols], in_=bank[:], func=ACT.Copy, scale=ngb_t[:, t : t + 1])
+            nc.sync.dma_start(n_cpy[t][:], n_win[t][:])
+
+        z_pl = keep.tile([P, PACK, S], BF16, name="z_pl", align_bytes=64)
+        for t in range(PACK):
+            for h in range(2):
+                nc.vector.tensor_copy(out=z_pl[:, t, halfcols(h)], in_=a_win[t][:].indirect(entries(n1_t, h * HALF, (h + 1) * HALF)))
+        shared = keep.tile([P, PACK * 1024], F32, name="shared", align_bytes=64)
+        z_il = shared[:, 1024:2048].bitcast(BF16)
+        nc.scalar.copy(
+            out=z_il.rearrange("p (u a i t) -> p a u i t", u=PACK, i=2, t=PACK),
+            in_=z_pl[:].rearrange("p t (a i u) -> p a u i t", u=PACK, i=2),
+        )
+        z_w = keep.tile([P, S], U32, name="z_w", align_bytes=64)
+        z_s = keep.tile([P, S], U8, name="z_s", align_bytes=64)
+
+        d_pl0 = keep.tile([P, PACK, HALF], F32, name="d_pl0")
+        d_il1 = keep.tile([P, PACK * HALF], BF16, name="d_il1", align_bytes=64)
+        d_pl = [d_pl0[:], shared[:].rearrange("p (t x) -> p t x", t=PACK)[:, :, 0:HALF]]
+        d_il = [shared[:, 2048:2560].bitcast(BF16), d_il1[:]]
+        d_w = [keep.tile([P, HALF], U32, name="d_w%d" % h, align_bytes=64) for h in range(2)]
+        d_s = [keep.tile([P, HALF], U8, name="d_s%d" % h, align_bytes=64) for h in range(2)]
+
+        def gather_z2(t, h, c0=0, c1=HALF):
+            nc.vector.tensor_tensor(
+                out=d_pl[h][:, t, c0:c1], in0=n_win[t][:].indirect(entries(n2_t, h * HALF + c0, h * HALF + c1)),
+                in1=n_cpy[t][:, h * HALF + c0 : h * HALF + c1], op=ALU.subtract,
+            )
+
+        def weave(copy, dst, src, c0, c1):
+            copy(
+                out=dst[:, PACK * c0 : PACK * c1].rearrange("p (c i t) -> p c t i", i=4, t=PACK),
+                in_=src[:, :, c0:c1].rearrange("p t (c i) -> p c t i", i=4),
+            )
+
+        s_win = [keep.tile([P, S], F32, name="s_win%d" % u) for u in range(PACK)]
+        s_cpy = [[keep.tile([P, HALF], F32, name="s_cpy%d_%d" % (u, h)) for h in range(2)] for u in range(PACK)]
+
+        def second_product(h):
+            for u in range(PACK):
+                rows = slice(u * P, (u + 1) * P)
+                bank = psum.tile([P, HALF], F32, name="bank", tag="bank")
+                nc.tensor.matmul_mx(
+                    out=bank[:], lhsT=z_w[:, rows].bitcast(FP8X4), lhsT_scale=z_s[:, rows],
+                    rhs=d_w[h][:].bitcast(FP8X4), rhs_scale=d_s[h][:], start=True, stop=True,
+                )
+                nc.scalar.activation(out=s_win[u][:, halfcols(h)], in_=bank[:], func=ACT.Copy, scale=0.0625)
+                if h == 1 or u >= 2:
+                    nc.sync.dma_start(s_cpy[u][h][:], s_win[u][:, halfcols(h)])
+
+        for t in range(PACK):
+            gather_z2(t, 0)
+        weave(nc.scalar.copy, d_il[0], d_pl[0], 0, HALF)
+        gather_z2(0, 1)
+        nc.vector.quantize_mx(out=z_w[:].bitcast(FP8X4), scales=z_s[:], in_=z_il)
+        gather_z2(1, 1)
+        nc.vector.quantize_mx(out=d_w[0][:].bitcast(FP8X4), scales=d_s[0][:], in_=d_il[0])
+        gather_z2(2, 1, 0, 128)
+        gather_z2(3, 1, 0, 128)
+        weave(nc.scalar.copy, d_il[1], d_pl[1], 0, 128)
+        gather_z2(2, 1, 128, 256)
+        gather_z2(3, 1, 128, 256)
+        weave(nc.vector.tensor_copy, d_il[1], d_pl[1], 128, HALF)
+        second_product(0)
+        nc.vector.quantize_mx(out=d_w[1][:].bitcast(FP8X4), scales=d_s[1][:], in_=d_il[1])
+        for u in range(2):
+            nc.vector.tensor_copy(out=s_cpy[u][0][:], in_=s_win[u][:, halfcols(0)])
+        second_product(1)
+
+        u_pl = [[keep.tile([P, HALF], F32, name="u_pl%d_%d" % (u, h)) for h in range(2)] for u in range(PACK)]
+        r_pl = [keep.tile([P, PACK, HALF], F32, name="r_pl%d" % h) for h in range(2)]
+        r_il = [keep.tile([P, PACK * HALF], BF16, name="r_il%d" % h, align_bytes=64) for h in range(2)]
+        r_w = [keep.tile([P, HALF], U32, name="r_w%d" % h, align_bytes=64) for h in range(2)]
+        r_s = keep.tile([P, S], U8, name="r_s", align_bytes=64)
+        out_rows = out_0.rearrange("(p u) j -> p u j", u=PACK)
+        out_words = out_1[0].rearrange("p n t -> p (n t)").bitcast(I32)
+
+        def gather_out(u, h, c0=0, c1=HALF):
+            nc.vector.tensor_tensor(
+                out=u_pl[u][h][:, c0:c1], in0=s_win[u][:].indirect(entries(cq_t, h * HALF + c0, h * HALF + c1)),
+                in1=s_cpy[u][h][:, c0:c1], op=ALU.add,
+            )
+            nc.scalar.activation(out=r_pl[h][:, u, c0:c1], in_=u_pl[u][h][:, c0:c1], func=ACT.Tanh)
+
+        def planes(h):
+            nc.vector.quantize_mx(out=r_w[h][:].bitcast(FP8X4), scales=r_s[:, halfcols(h)], in_=r_il[h][:])
+            nc.sync.dma_start(out_words[:, halfcols(h)], r_w[h][:].bitcast(I32))
+
+        for u in range(PACK):
+            gather_out(u, 0)
+        nc.sync.dma_start(out_rows[:, :, halfcols(0)], r_pl[0][:])
+        weave(nc.scalar.copy, r_il[0], r_pl[0], 0, HALF)
+        gather_out(0, 1)
+        gather_out(1, 1)
+        nc.sync.dma_start(out_rows[:, 0:2, halfcols(1)], r_pl[1][:, 0:2, :])
+        gather_out(2, 1, 0, 128)
+        gather_out(3, 1, 0, 128)
+        gather_out(2, 1, 128, 256)
+        gather_out(3, 1, 128, 256)
+        nc.sync.dma_start(out_rows[:, 2:4, halfcols(1)], r_pl[1][:, 2:4, :])
+        planes(0)
+        weave(nc.vector.tensor_copy, r_il[1], r_pl[1], 0, 128)
+        weave(nc.vector.tensor_copy, r_il[1], r_pl[1], 128, HALF)
+        planes(1)
+        for q in range(4):
+            queue = nc.sync if q % 2 == 0 else nc.scalar
+            queue.dma_start(out_2[0, 4 * q : 4 * q + 4, :].bitcast(I32), r_s[32 * q : 32 * q + 4, :].bitcast(I32))

@@ -17,6 +17,8 @@ PACK = 4
 T = 2048
 S = 512
 HALF = S // 2
+QUARTER = S // 4
+S_SCALE = 0.0625
 FLOPS = 2 * 2 * 512 * 512 * 512
 
 
@@ -28,7 +30,7 @@ def tile_picked_autoc8_none_po_kernel(
     def entries(list_tile, j0, j1):
         return list_tile[:, j0 // 16 : j1 // 16]
 
-    def halfcols(h):
+    def half(h):
         return slice(h * HALF, (h + 1) * HALF)
 
     with ExitStack() as ctx:
@@ -47,75 +49,93 @@ def tile_picked_autoc8_none_po_kernel(
         w_s = keep.tile([P, S], U8, name="w_s", align_bytes=64)
         ga_t = keep.tile([P, PACK], F32, name="ga_t")
         gb_t = keep.tile([P, PACK], F32, name="gb_t")
-        ngb_t = keep.tile([P, PACK], F32, name="ngb_t")
+        warm_in = keep.tile([P, 1], F32, name="warm_in")
         warm_out = keep.tile([P, 1], F32, name="warm_out")
 
-        nc.vector.memset(x_s[:].bitcast(I32), 0)
+        nc.vector.memset(x_s[0:112, :].bitcast(I32), 0)
         nc.gpsimd.memset(w_s[:].bitcast(I32), 0)
+        nc.vector.memset(warm_in[:], 0.0)
+        nc.scalar.activation(out=warm_out[:], in_=warm_in[:], func=ACT.Tanh)
 
-        def load_scale_rows(queue, plane, scales, q):
-            queue.dma_start(plane[32 * q : 32 * q + 4, :].bitcast(I32), scales[0, 4 * q : 4 * q + 4, :].bitcast(I32))
-
+        nc.sync.dma_start(x_s[112:128, :].bitcast(I32), x_scales[0].bitcast(I32))
         nc.sync.dma_start(offs_t[:], offs)
         nc.sync.dma_start(n1_t[:], n1)
         nc.sync.dma_start(n2_t[:], n2)
         nc.sync.dma_start(cq_t[:], cq)
         nc.sync.dma_start(w_w[:].bitcast(I32), w1_words[0].rearrange("p n t -> p (n t)").bitcast(I32))
+        nc.sync.dma_start(w_s[0:16, :].bitcast(I32), w1_scales[0].bitcast(I32))
         nc.sync.dma_start(x_w[:].bitcast(I32), x_words[0].rearrange("p n t -> p (n t)").bitcast(I32))
-        for q in range(4):
-            load_scale_rows(nc.scalar, x_s, x_scales, q)
-        for q in range(2):
-            load_scale_rows(nc.scalar, w_s, w1_scales, q)
         nc.gpsimd.dma_start(ga_t[:], ga.rearrange("(p t) o -> p (t o)", t=PACK))
-        for q in range(2, 4):
-            load_scale_rows(nc.gpsimd, w_s, w1_scales, q)
         nc.gpsimd.dma_start(gb_t[:], gb.rearrange("(p t) o -> p (t o)", t=PACK))
-        nc.scalar.activation(out=warm_out[:], in_=ga_t[:, 0:1], func=ACT.Tanh)
-
-        nc.gpsimd.tensor_scalar(out=ngb_t[:], in0=gb_t[:], scalar1=-1.0, scalar2=0.0, op0=ALU.mult, op1=ALU.add)
 
         wd_w = keep.tile([P, S], U32, name="wd_w", align_bytes=64)
         wd_s = keep.tile([P, S], U8, name="wd_s", align_bytes=64)
-        nc.vector.tensor_copy(
-            out=wd_w[:].rearrange("p (t a i) -> p a t i", t=PACK, i=4),
-            in_=w_w[:].rearrange("p (a i t) -> p a t i", t=PACK, i=4),
-        )
+        xg_rows = keep.tile([P, S], U8, name="xg_rows", align_bytes=64)
         xg_s = keep.tile([P, S], U8, name="xg_s", align_bytes=64)
-        nc.vector.tensor_copy(out=xg_s[:], in_=x_s[:].indirect(offs_t[:]))
+        xg_w = keep.tile([P, S], U32, name="xg_w", align_bytes=64)
+
+        def place_rows(queue, plane, rows, first, q):
+            queue.dma_start(plane[32 * q : 32 * q + 4, :].bitcast(I32), rows[first + 4 * q : first + 4 * q + 4, :].bitcast(I32))
+
+        nc.vector.tensor_copy(out=xg_rows[:], in_=x_s[:].indirect(offs_t[:]))
+        for q in range(4):
+            place_rows(nc.sync, xg_s, xg_rows, 112, q)
         nc.vector.tensor_copy(
             out=wd_s[:].rearrange("p (t a i) -> p a t i", t=PACK, i=16),
             in_=w_s[:].rearrange("p (a i t) -> p a t i", t=PACK, i=16),
         )
-        xg_w = keep.tile([P, S], U32, name="xg_w", align_bytes=64)
+        for q in range(1, 4):
+            place_rows(nc.scalar, wd_s, wd_s, 0, q)
+        nc.vector.tensor_copy(
+            out=wd_w[:].rearrange("p (t a i) -> p a t i", t=PACK, i=4),
+            in_=w_w[:].rearrange("p (a i t) -> p a t i", t=PACK, i=4),
+        )
         for h in range(2):
-            nc.vector.tensor_copy(out=xg_w[:, halfcols(h)], in_=x_w[:].indirect(entries(offs_t, h * HALF, (h + 1) * HALF)))
+            nc.vector.tensor_copy(out=xg_w[:, half(h)], in_=x_w[:].indirect(entries(offs_t, h * HALF, (h + 1) * HALF)))
+
+        def product(cols, lhs_w, lhs_s, rhs_w, rhs_s):
+            bank = psum.tile([P, cols], F32, name="bank", tag="bank")
+            nc.tensor.matmul_mx(
+                out=bank[:], lhsT=lhs_w.bitcast(FP8X4), lhsT_scale=lhs_s,
+                rhs=rhs_w.bitcast(FP8X4), rhs_scale=rhs_s, start=True, stop=True,
+            )
+            return bank
+
+        def block(t):
+            return slice(t * P, (t + 1) * P)
+
+        def scaled(out, in_, scale):
+            nc.scalar.activation(out=out, in_=in_, func=ACT.Copy, scale=scale)
+
+        y0 = [product(HALF, wd_w[:, block(0)], wd_s[:, block(0)], xg_w[:, half(h)], xg_s[:, half(h)]) for h in range(2)]
+        y = [None] + [product(S, wd_w[:, block(t)], wd_s[:, block(t)], xg_w[:], xg_s[:]) for t in range(1, PACK)]
 
         a_win = [keep.tile([P, S], F32, name="a_win%d" % t) for t in range(PACK)]
-        n_win = [keep.tile([P, S], F32, name="n_win%d" % t) for t in range(PACK)]
-        n_cpy = [keep.tile([P, S], F32, name="n_cpy%d" % t) for t in range(PACK)]
-        for t in range(PACK):
-            rows = slice(t * P, (t + 1) * P)
-            pieces = [halfcols(0), halfcols(1)] if t == 0 else [slice(0, S)]
-            banks = []
-            for cols in pieces:
-                bank = psum.tile([P, cols.stop - cols.start], F32, name="bank", tag="bank")
-                nc.tensor.matmul_mx(
-                    out=bank[:], lhsT=wd_w[:, rows].bitcast(FP8X4), lhsT_scale=wd_s[:, rows],
-                    rhs=xg_w[:, cols].bitcast(FP8X4), rhs_scale=xg_s[:, cols], start=True, stop=True,
-                )
-                banks.append(bank)
-            for cols, bank in zip(pieces, banks):
-                nc.scalar.activation(out=a_win[t][:, cols], in_=bank[:], func=ACT.Copy, scale=ga_t[:, t : t + 1])
-            for cols, bank in zip(pieces, banks):
-                nc.scalar.activation(out=n_win[t][:, cols], in_=bank[:], func=ACT.Copy, scale=ngb_t[:, t : t + 1])
-            nc.sync.dma_start(n_cpy[t][:], n_win[t][:])
+        b_win = [keep.tile([P, S], F32, name="b_win%d" % t) for t in range(PACK)]
+        shared = keep.tile([P, 1280], F32, name="shared", align_bytes=64)
+        b_cpy = [keep.tile([P, S], F32, name="b_cpy%d" % t) for t in range(PACK - 1)]
+        b_last = keep.tile([P, HALF], F32, name="b_last")
+        b_other = [[c[:, half(0)], c[:, half(1)]] for c in b_cpy] + [[shared[:, 0:HALF], b_last[:]]]
+
+        for h in range(2):
+            nc.vector.tensor_scalar(out=a_win[0][:, half(h)], in0=y0[h][:], scalar1=ga_t[:, 0:1], scalar2=None, op0=ALU.mult)
+            scaled(b_win[0][:, half(h)], y0[h][:], gb_t[:, 0:1])
+        nc.sync.dma_start(b_cpy[0][:], b_win[0][:])
+        scaled(a_win[1][:], y[1][:], ga_t[:, 1:2])
+        for t in range(1, PACK):
+            if t + 1 < PACK:
+                scaled(a_win[t + 1][:], y[t + 1][:], ga_t[:, t + 1 : t + 2])
+            scaled(b_win[t][:], y[t][:], gb_t[:, t : t + 1])
+            if t + 1 < PACK:
+                nc.sync.dma_start(b_cpy[t][:], b_win[t][:])
+        nc.sync.dma_start(b_other[3][1], b_win[3][:, half(1)])
+        scaled(b_other[3][0], y[3][:, half(0)], gb_t[:, 3:4])
 
         z_pl = keep.tile([P, PACK, S], BF16, name="z_pl", align_bytes=64)
         for t in range(PACK):
             for h in range(2):
-                nc.vector.tensor_copy(out=z_pl[:, t, halfcols(h)], in_=a_win[t][:].indirect(entries(n1_t, h * HALF, (h + 1) * HALF)))
-        shared = keep.tile([P, PACK * 1024], F32, name="shared", align_bytes=64)
-        z_il = shared[:, 1024:2048].bitcast(BF16)
+                nc.vector.tensor_copy(out=z_pl[:, t, half(h)], in_=a_win[t][:].indirect(entries(n1_t, h * HALF, (h + 1) * HALF)))
+        z_il = shared[:, HALF:1280].bitcast(BF16)
         nc.scalar.copy(
             out=z_il.rearrange("p (u a i t) -> p a u i t", u=PACK, i=2, t=PACK),
             in_=z_pl[:].rearrange("p t (a i u) -> p a u i t", u=PACK, i=2),
@@ -124,61 +144,59 @@ def tile_picked_autoc8_none_po_kernel(
         z_s = keep.tile([P, S], U8, name="z_s", align_bytes=64)
 
         d_pl0 = keep.tile([P, PACK, HALF], F32, name="d_pl0")
-        d_il1 = keep.tile([P, PACK * HALF], BF16, name="d_il1", align_bytes=64)
-        d_pl = [d_pl0[:], shared[:].rearrange("p (t x) -> p t x", t=PACK)[:, :, 0:HALF]]
-        d_il = [shared[:, 2048:2560].bitcast(BF16), d_il1[:]]
+        d_pl = [d_pl0[:], shared[:, 0:1024].rearrange("p (t x) -> p t x", t=PACK)]
+        d_il = [keep.tile([P, PACK * HALF], BF16, name="d_il%d" % h, align_bytes=64)[:] for h in range(2)]
         d_w = [keep.tile([P, HALF], U32, name="d_w%d" % h, align_bytes=64) for h in range(2)]
         d_s = [keep.tile([P, HALF], U8, name="d_s%d" % h, align_bytes=64) for h in range(2)]
 
         def gather_z2(t, h, c0=0, c1=HALF):
             nc.vector.tensor_tensor(
-                out=d_pl[h][:, t, c0:c1], in0=n_win[t][:].indirect(entries(n2_t, h * HALF + c0, h * HALF + c1)),
-                in1=n_cpy[t][:, h * HALF + c0 : h * HALF + c1], op=ALU.subtract,
+                out=d_pl[h][:, t, c0:c1], in0=b_win[t][:].indirect(entries(n2_t, h * HALF + c0, h * HALF + c1)),
+                in1=b_other[t][h][:, c0:c1], op=ALU.subtract,
             )
 
-        def weave(copy, dst, src, c0, c1):
-            copy(
-                out=dst[:, PACK * c0 : PACK * c1].rearrange("p (c i t) -> p c t i", i=4, t=PACK),
-                in_=src[:, :, c0:c1].rearrange("p t (c i) -> p c t i", i=4),
-            )
+        def woven(dst, c0, c1):
+            return dst[:, PACK * c0 : PACK * c1].rearrange("p (c i t) -> p c t i", i=4, t=PACK)
+
+        def planar(src, c0, c1):
+            return src[:, :, c0:c1].rearrange("p t (c i) -> p c t i", i=4)
 
         s_win = [keep.tile([P, S], F32, name="s_win%d" % u) for u in range(PACK)]
-        s_cpy = [[keep.tile([P, HALF], F32, name="s_cpy%d_%d" % (u, h)) for h in range(2)] for u in range(PACK)]
-
-        def second_product(h):
-            for u in range(PACK):
-                rows = slice(u * P, (u + 1) * P)
-                bank = psum.tile([P, HALF], F32, name="bank", tag="bank")
-                nc.tensor.matmul_mx(
-                    out=bank[:], lhsT=z_w[:, rows].bitcast(FP8X4), lhsT_scale=z_s[:, rows],
-                    rhs=d_w[h][:].bitcast(FP8X4), rhs_scale=d_s[h][:], start=True, stop=True,
-                )
-                nc.scalar.activation(out=s_win[u][:, halfcols(h)], in_=bank[:], func=ACT.Copy, scale=0.0625)
-                if h == 1 or u >= 2:
-                    nc.sync.dma_start(s_cpy[u][h][:], s_win[u][:, halfcols(h)])
+        shared2 = keep.tile([P, 2 * HALF], F32, name="shared2", align_bytes=64)
+        s_cpy = [[keep.tile([P, HALF], F32, name="s_cpy%d_%d" % (u, h))[:] for h in range(2) if (u, h) != (3, 1)] for u in range(PACK)]
+        s_cpy[3].append(shared2[:, HALF : 2 * HALF])
 
         for t in range(PACK):
             gather_z2(t, 0)
-        weave(nc.scalar.copy, d_il[0], d_pl[0], 0, HALF)
+        nc.vector.tensor_scalar(out=woven(d_il[0], 0, HALF), in0=planar(d_pl[0], 0, HALF), scalar1=-1.0, scalar2=None, op0=ALU.mult)
         gather_z2(0, 1)
-        nc.vector.quantize_mx(out=z_w[:].bitcast(FP8X4), scales=z_s[:], in_=z_il)
-        gather_z2(1, 1)
         nc.vector.quantize_mx(out=d_w[0][:].bitcast(FP8X4), scales=d_s[0][:], in_=d_il[0])
-        gather_z2(2, 1, 0, 128)
-        gather_z2(3, 1, 0, 128)
-        weave(nc.scalar.copy, d_il[1], d_pl[1], 0, 128)
-        gather_z2(2, 1, 128, 256)
-        gather_z2(3, 1, 128, 256)
-        weave(nc.vector.tensor_copy, d_il[1], d_pl[1], 128, HALF)
-        second_product(0)
+        nc.vector.quantize_mx(out=z_w[:].bitcast(FP8X4), scales=z_s[:], in_=z_il)
+        s0 = [product(HALF, z_w[:, block(u)], z_s[:, block(u)], d_w[0][:], d_s[0][:]) for u in range(PACK)]
+        for t in range(1, PACK):
+            gather_z2(t, 1)
+        nc.vector.tensor_scalar(out=woven(d_il[1], 0, HALF), in0=planar(d_pl[1], 0, HALF), scalar1=-1.0, scalar2=None, op0=ALU.mult)
         nc.vector.quantize_mx(out=d_w[1][:].bitcast(FP8X4), scales=d_s[1][:], in_=d_il[1])
-        for u in range(2):
-            nc.vector.tensor_copy(out=s_cpy[u][0][:], in_=s_win[u][:, halfcols(0)])
-        second_product(1)
+        s1 = [product(HALF, z_w[:, block(u)], z_s[:, block(u)], d_w[1][:], d_s[1][:]) for u in range(PACK)]
 
-        u_pl = [[keep.tile([P, HALF], F32, name="u_pl%d_%d" % (u, h)) for h in range(2)] for u in range(PACK)]
+        def evacuate(u, h):
+            if (u, h) == (0, 1):
+                nc.vector.tensor_scalar(out=s_win[u][:, half(h)], in0=s1[u][:], scalar1=S_SCALE, scalar2=None, op0=ALU.mult)
+            else:
+                scaled(s_win[u][:, half(h)], (s0, s1)[h][u][:], S_SCALE)
+            if h == 0 and u == 0:
+                nc.vector.tensor_copy(out=s_cpy[u][0], in_=s_win[u][:, half(0)])
+            else:
+                nc.sync.dma_start(s_cpy[u][h], s_win[u][:, half(h)])
+
+        for h in range(2):
+            for u in range(PACK):
+                evacuate(u, h)
+
+        u_pl = [keep.tile([P, PACK, HALF], F32, name="u_pl%d" % h) for h in range(2)]
         r_pl = [keep.tile([P, PACK, HALF], F32, name="r_pl%d" % h) for h in range(2)]
-        r_il = [keep.tile([P, PACK * HALF], BF16, name="r_il%d" % h, align_bytes=64) for h in range(2)]
+        r_il1 = keep.tile([P, PACK * HALF], BF16, name="r_il1", align_bytes=64)
+        r_il = [shared2[:].bitcast(BF16), r_il1[:]]
         r_w = [keep.tile([P, HALF], U32, name="r_w%d" % h, align_bytes=64) for h in range(2)]
         r_s = keep.tile([P, S], U8, name="r_s", align_bytes=64)
         out_rows = out_0.rearrange("(p u) j -> p u j", u=PACK)
@@ -186,30 +204,40 @@ def tile_picked_autoc8_none_po_kernel(
 
         def gather_out(u, h, c0=0, c1=HALF):
             nc.vector.tensor_tensor(
-                out=u_pl[u][h][:, c0:c1], in0=s_win[u][:].indirect(entries(cq_t, h * HALF + c0, h * HALF + c1)),
+                out=u_pl[h][:, u, c0:c1], in0=s_win[u][:].indirect(entries(cq_t, h * HALF + c0, h * HALF + c1)),
                 in1=s_cpy[u][h][:, c0:c1], op=ALU.add,
             )
-            nc.scalar.activation(out=r_pl[h][:, u, c0:c1], in_=u_pl[u][h][:, c0:c1], func=ACT.Tanh)
+
+        def tanh_pair(u, h, c0=0, c1=HALF):
+            nc.scalar.activation(out=r_pl[h][:, u : u + 2, c0:c1], in_=u_pl[h][:, u : u + 2, c0:c1], func=ACT.Tanh)
+
+        def store_pair(queue, u, h, c0=0, c1=HALF):
+            queue.dma_start(out_rows[:, u : u + 2, h * HALF + c0 : h * HALF + c1], r_pl[h][:, u : u + 2, c0:c1])
 
         def planes(h):
-            nc.vector.quantize_mx(out=r_w[h][:].bitcast(FP8X4), scales=r_s[:, halfcols(h)], in_=r_il[h][:])
-            nc.sync.dma_start(out_words[:, halfcols(h)], r_w[h][:].bitcast(I32))
+            nc.vector.quantize_mx(out=r_w[h][:].bitcast(FP8X4), scales=r_s[:, half(h)], in_=r_il[h])
+            nc.sync.dma_start(out_words[:, half(h)], r_w[h][:].bitcast(I32))
 
-        for u in range(PACK):
+        for u in range(0, PACK, 2):
             gather_out(u, 0)
-        nc.sync.dma_start(out_rows[:, :, halfcols(0)], r_pl[0][:])
-        weave(nc.scalar.copy, r_il[0], r_pl[0], 0, HALF)
+            gather_out(u + 1, 0)
+            tanh_pair(u, 0)
+            store_pair(nc.sync, u, 0)
+        nc.scalar.copy(out=woven(r_il[0], 0, QUARTER), in_=planar(r_pl[0], 0, QUARTER))
         gather_out(0, 1)
         gather_out(1, 1)
-        nc.sync.dma_start(out_rows[:, 0:2, halfcols(1)], r_pl[1][:, 0:2, :])
-        gather_out(2, 1, 0, 128)
-        gather_out(3, 1, 0, 128)
-        gather_out(2, 1, 128, 256)
-        gather_out(3, 1, 128, 256)
-        nc.sync.dma_start(out_rows[:, 2:4, halfcols(1)], r_pl[1][:, 2:4, :])
+        tanh_pair(0, 1)
+        store_pair(nc.sync, 0, 1)
+        for c0 in (0, QUARTER):
+            gather_out(2, 1, c0, c0 + QUARTER)
+            gather_out(3, 1, c0, c0 + QUARTER)
+            if c0 == QUARTER:
+                nc.scalar.activation(out=woven(r_il[1], QUARTER, HALF), in_=planar(u_pl[1], QUARTER, HALF), func=ACT.Tanh)
+            tanh_pair(2, 1, c0, c0 + QUARTER)
+            store_pair(nc.sync, 2, 1, c0, c0 + QUARTER)
+        nc.vector.tensor_copy(out=woven(r_il[0], QUARTER, HALF), in_=planar(r_pl[0], QUARTER, HALF))
         planes(0)
-        weave(nc.vector.tensor_copy, r_il[1], r_pl[1], 0, 128)
-        weave(nc.vector.tensor_copy, r_il[1], r_pl[1], 128, HALF)
+        nc.vector.tensor_copy(out=woven(r_il[1], 0, QUARTER), in_=planar(r_pl[1], 0, QUARTER))
         planes(1)
         for q in range(4):
             queue = nc.sync if q % 2 == 0 else nc.scalar

from contextlib import ExitStack

import concourse.mybir as mybir

F32 = mybir.dt.float32
BF16 = mybir.dt.bfloat16
I32 = mybir.dt.int32
U32 = mybir.dt.uint32
U16 = mybir.dt.uint16
U8 = mybir.dt.uint8
FP8X4 = mybir.dt.float8_e4m3fn_x4
ALU = mybir.AluOpType
ACT = mybir.ActivationFunctionType

P = 128
PACK = 4
T = 2048
S = 512
HALF = S // 2
QUARTER = S // 4
S_SCALE = 0.0625
FLOPS = 2 * 2 * 512 * 512 * 512


def tile_picked_autoc8_none_po_kernel(
    tc, x_words, x_scales, w1_words, w1_scales, ga, gb, offs, n1, n2, cq, out_0, out_1, out_2
):
    nc = tc.nc

    def entries(list_tile, j0, j1):
        return list_tile[:, j0 // 16 : j1 // 16]

    def half(h):
        return slice(h * HALF, (h + 1) * HALF)

    with ExitStack() as ctx:
        lists = ctx.enter_context(tc.tile_pool(name="lists", bufs=1))
        keep = ctx.enter_context(tc.tile_pool(name="keep", bufs=1))
        psum = ctx.enter_context(tc.psum_pool(name="psum", bufs=8))

        offs_t = lists.tile([P, S // 16], U16, name="offs_t")
        n1_t = lists.tile([P, S // 16], U16, name="n1_t")
        n2_t = lists.tile([P, S // 16], U16, name="n2_t")
        cq_t = lists.tile([P, S // 16], U16, name="cq_t")

        x_w = keep.tile([P, T], U32, name="x_w", align_bytes=64)
        x_s = keep.tile([P, T], U8, name="x_s", align_bytes=64)
        w_w = keep.tile([P, S], U32, name="w_w", align_bytes=64)
        w_s = keep.tile([P, S], U8, name="w_s", align_bytes=64)
        ga_t = keep.tile([P, PACK], F32, name="ga_t")
        gb_t = keep.tile([P, PACK], F32, name="gb_t")
        warm_in = keep.tile([P, 1], F32, name="warm_in")
        warm_out = keep.tile([P, 1], F32, name="warm_out")

        nc.vector.memset(x_s[0:112, :].bitcast(I32), 0)
        nc.gpsimd.memset(w_s[:].bitcast(I32), 0)
        nc.vector.memset(warm_in[:], 0.0)
        nc.scalar.activation(out=warm_out[:], in_=warm_in[:], func=ACT.Tanh)

        nc.sync.dma_start(x_s[112:128, :].bitcast(I32), x_scales[0].bitcast(I32))
        nc.sync.dma_start(offs_t[:], offs)
        nc.sync.dma_start(n1_t[:], n1)
        nc.sync.dma_start(n2_t[:], n2)
        nc.sync.dma_start(cq_t[:], cq)
        nc.sync.dma_start(w_w[:].bitcast(I32), w1_words[0].rearrange("p n t -> p (n t)").bitcast(I32))
        nc.sync.dma_start(w_s[0:16, :].bitcast(I32), w1_scales[0].bitcast(I32))
        nc.sync.dma_start(x_w[:].bitcast(I32), x_words[0].rearrange("p n t -> p (n t)").bitcast(I32))
        nc.gpsimd.dma_start(ga_t[:], ga.rearrange("(p t) o -> p (t o)", t=PACK))
        nc.gpsimd.dma_start(gb_t[:], gb.rearrange("(p t) o -> p (t o)", t=PACK))

        wd_w = keep.tile([P, S], U32, name="wd_w", align_bytes=64)
        wd_s = keep.tile([P, S], U8, name="wd_s", align_bytes=64)
        xg_rows = keep.tile([P, S], U8, name="xg_rows", align_bytes=64)
        xg_s = keep.tile([P, S], U8, name="xg_s", align_bytes=64)
        xg_w = keep.tile([P, S], U32, name="xg_w", align_bytes=64)

        def place_rows(queue, plane, rows, first, q):
            queue.dma_start(plane[32 * q : 32 * q + 4, :].bitcast(I32), rows[first + 4 * q : first + 4 * q + 4, :].bitcast(I32))

        nc.vector.tensor_copy(out=xg_rows[:], in_=x_s[:].indirect(offs_t[:]))
        for q in range(4):
            place_rows(nc.sync, xg_s, xg_rows, 112, q)
        nc.vector.tensor_copy(
            out=wd_s[:].rearrange("p (t a i) -> p a t i", t=PACK, i=16),
            in_=w_s[:].rearrange("p (a i t) -> p a t i", t=PACK, i=16),
        )
        for q in range(1, 4):
            place_rows(nc.scalar, wd_s, wd_s, 0, q)
        nc.vector.tensor_copy(
            out=wd_w[:].rearrange("p (t a i) -> p a t i", t=PACK, i=4),
            in_=w_w[:].rearrange("p (a i t) -> p a t i", t=PACK, i=4),
        )
        for h in range(2):
            nc.vector.tensor_copy(out=xg_w[:, half(h)], in_=x_w[:].indirect(entries(offs_t, h * HALF, (h + 1) * HALF)))

        def product(cols, lhs_w, lhs_s, rhs_w, rhs_s):
            bank = psum.tile([P, cols], F32, name="bank", tag="bank")
            nc.tensor.matmul_mx(
                out=bank[:], lhsT=lhs_w.bitcast(FP8X4), lhsT_scale=lhs_s,
                rhs=rhs_w.bitcast(FP8X4), rhs_scale=rhs_s, start=True, stop=True,
            )
            return bank

        def block(t):
            return slice(t * P, (t + 1) * P)

        def scaled(out, in_, scale):
            nc.scalar.activation(out=out, in_=in_, func=ACT.Copy, scale=scale)

        y0 = [product(HALF, wd_w[:, block(0)], wd_s[:, block(0)], xg_w[:, half(h)], xg_s[:, half(h)]) for h in range(2)]
        y = [None] + [product(S, wd_w[:, block(t)], wd_s[:, block(t)], xg_w[:], xg_s[:]) for t in range(1, PACK)]

        a_win = [keep.tile([P, S], F32, name="a_win%d" % t) for t in range(PACK)]
        b_win = [keep.tile([P, S], F32, name="b_win%d" % t) for t in range(PACK)]
        shared = keep.tile([P, 1280], F32, name="shared", align_bytes=64)
        b_cpy = [keep.tile([P, S], F32, name="b_cpy%d" % t) for t in range(PACK - 1)]
        b_last = keep.tile([P, HALF], F32, name="b_last")
        b_other = [[c[:, half(0)], c[:, half(1)]] for c in b_cpy] + [[shared[:, 0:HALF], b_last[:]]]

        for h in range(2):
            nc.vector.tensor_scalar(out=a_win[0][:, half(h)], in0=y0[h][:], scalar1=ga_t[:, 0:1], scalar2=None, op0=ALU.mult)
            scaled(b_win[0][:, half(h)], y0[h][:], gb_t[:, 0:1])
        nc.sync.dma_start(b_cpy[0][:], b_win[0][:])
        scaled(a_win[1][:], y[1][:], ga_t[:, 1:2])
        for t in range(1, PACK):
            if t + 1 < PACK:
                scaled(a_win[t + 1][:], y[t + 1][:], ga_t[:, t + 1 : t + 2])
            scaled(b_win[t][:], y[t][:], gb_t[:, t : t + 1])
            if t + 1 < PACK:
                nc.sync.dma_start(b_cpy[t][:], b_win[t][:])
        nc.sync.dma_start(b_other[3][1], b_win[3][:, half(1)])
        scaled(b_other[3][0], y[3][:, half(0)], gb_t[:, 3:4])

        z_pl = keep.tile([P, PACK, S], BF16, name="z_pl", align_bytes=64)
        for t in range(PACK):
            for h in range(2):
                nc.vector.tensor_copy(out=z_pl[:, t, half(h)], in_=a_win[t][:].indirect(entries(n1_t, h * HALF, (h + 1) * HALF)))
        z_il = shared[:, HALF:1280].bitcast(BF16)
        nc.scalar.copy(
            out=z_il.rearrange("p (u a i t) -> p a u i t", u=PACK, i=2, t=PACK),
            in_=z_pl[:].rearrange("p t (a i u) -> p a u i t", u=PACK, i=2),
        )
        z_w = keep.tile([P, S], U32, name="z_w", align_bytes=64)
        z_s = keep.tile([P, S], U8, name="z_s", align_bytes=64)

        d_pl0 = keep.tile([P, PACK, HALF], F32, name="d_pl0")
        d_pl = [d_pl0[:], shared[:, 0:1024].rearrange("p (t x) -> p t x", t=PACK)]
        d_il = [keep.tile([P, PACK * HALF], BF16, name="d_il%d" % h, align_bytes=64)[:] for h in range(2)]
        d_w = [keep.tile([P, HALF], U32, name="d_w%d" % h, align_bytes=64) for h in range(2)]
        d_s = [keep.tile([P, HALF], U8, name="d_s%d" % h, align_bytes=64) for h in range(2)]

        def gather_z2(t, h, c0=0, c1=HALF):
            nc.vector.tensor_tensor(
                out=d_pl[h][:, t, c0:c1], in0=b_win[t][:].indirect(entries(n2_t, h * HALF + c0, h * HALF + c1)),
                in1=b_other[t][h][:, c0:c1], op=ALU.subtract,
            )

        def woven(dst, c0, c1):
            return dst[:, PACK * c0 : PACK * c1].rearrange("p (c i t) -> p c t i", i=4, t=PACK)

        def planar(src, c0, c1):
            return src[:, :, c0:c1].rearrange("p t (c i) -> p c t i", i=4)

        s_win = [keep.tile([P, S], F32, name="s_win%d" % u) for u in range(PACK)]
        shared2 = keep.tile([P, 2 * HALF], F32, name="shared2", align_bytes=64)
        s_cpy = [[keep.tile([P, HALF], F32, name="s_cpy%d_%d" % (u, h))[:] for h in range(2) if (u, h) != (3, 1)] for u in range(PACK)]
        s_cpy[3].append(shared2[:, HALF : 2 * HALF])

        for t in range(PACK):
            gather_z2(t, 0)
        nc.vector.tensor_scalar(out=woven(d_il[0], 0, HALF), in0=planar(d_pl[0], 0, HALF), scalar1=-1.0, scalar2=None, op0=ALU.mult)
        gather_z2(0, 1)
        nc.vector.quantize_mx(out=d_w[0][:].bitcast(FP8X4), scales=d_s[0][:], in_=d_il[0])
        nc.vector.quantize_mx(out=z_w[:].bitcast(FP8X4), scales=z_s[:], in_=z_il)
        s0 = [product(HALF, z_w[:, block(u)], z_s[:, block(u)], d_w[0][:], d_s[0][:]) for u in range(PACK)]
        for t in range(1, PACK):
            gather_z2(t, 1)
        nc.vector.tensor_scalar(out=woven(d_il[1], 0, HALF), in0=planar(d_pl[1], 0, HALF), scalar1=-1.0, scalar2=None, op0=ALU.mult)
        nc.vector.quantize_mx(out=d_w[1][:].bitcast(FP8X4), scales=d_s[1][:], in_=d_il[1])
        s1 = [product(HALF, z_w[:, block(u)], z_s[:, block(u)], d_w[1][:], d_s[1][:]) for u in range(PACK)]

        def evacuate(u, h):
            if (u, h) == (0, 1):
                nc.vector.tensor_scalar(out=s_win[u][:, half(h)], in0=s1[u][:], scalar1=S_SCALE, scalar2=None, op0=ALU.mult)
            else:
                scaled(s_win[u][:, half(h)], (s0, s1)[h][u][:], S_SCALE)
            if h == 0 and u == 0:
                nc.vector.tensor_copy(out=s_cpy[u][0], in_=s_win[u][:, half(0)])
            else:
                nc.sync.dma_start(s_cpy[u][h], s_win[u][:, half(h)])

        for h in range(2):
            for u in range(PACK):
                evacuate(u, h)

        u_pl = [keep.tile([P, PACK, HALF], F32, name="u_pl%d" % h) for h in range(2)]
        r_pl = [keep.tile([P, PACK, HALF], F32, name="r_pl%d" % h) for h in range(2)]
        r_il1 = keep.tile([P, PACK * HALF], BF16, name="r_il1", align_bytes=64)
        r_il = [shared2[:].bitcast(BF16), r_il1[:]]
        r_w = [keep.tile([P, HALF], U32, name="r_w%d" % h, align_bytes=64) for h in range(2)]
        r_s = keep.tile([P, S], U8, name="r_s", align_bytes=64)
        out_rows = out_0.rearrange("(p u) j -> p u j", u=PACK)
        out_words = out_1[0].rearrange("p n t -> p (n t)").bitcast(I32)

        def gather_out(u, h, c0=0, c1=HALF):
            nc.vector.tensor_tensor(
                out=u_pl[h][:, u, c0:c1], in0=s_win[u][:].indirect(entries(cq_t, h * HALF + c0, h * HALF + c1)),
                in1=s_cpy[u][h][:, c0:c1], op=ALU.add,
            )

        def tanh_pair(u, h, c0=0, c1=HALF):
            nc.scalar.activation(out=r_pl[h][:, u : u + 2, c0:c1], in_=u_pl[h][:, u : u + 2, c0:c1], func=ACT.Tanh)

        def store_pair(queue, u, h, c0=0, c1=HALF):
            queue.dma_start(out_rows[:, u : u + 2, h * HALF + c0 : h * HALF + c1], r_pl[h][:, u : u + 2, c0:c1])

        def planes(h):
            nc.vector.quantize_mx(out=r_w[h][:].bitcast(FP8X4), scales=r_s[:, half(h)], in_=r_il[h])
            nc.sync.dma_start(out_words[:, half(h)], r_w[h][:].bitcast(I32))

        for u in range(0, PACK, 2):
            gather_out(u, 0)
            gather_out(u + 1, 0)
            tanh_pair(u, 0)
            store_pair(nc.sync, u, 0)
        nc.scalar.copy(out=woven(r_il[0], 0, QUARTER), in_=planar(r_pl[0], 0, QUARTER))
        gather_out(0, 1)
        gather_out(1, 1)
        tanh_pair(0, 1)
        store_pair(nc.sync, 0, 1)
        for c0 in (0, QUARTER):
            gather_out(2, 1, c0, c0 + QUARTER)
            gather_out(3, 1, c0, c0 + QUARTER)
            if c0 == QUARTER:
                nc.scalar.activation(out=woven(r_il[1], QUARTER, HALF), in_=planar(u_pl[1], QUARTER, HALF), func=ACT.Tanh)
            tanh_pair(2, 1, c0, c0 + QUARTER)
            store_pair(nc.sync, 2, 1, c0, c0 + QUARTER)
        nc.vector.tensor_copy(out=woven(r_il[0], QUARTER, HALF), in_=planar(r_pl[0], QUARTER, HALF))
        planes(0)
        nc.vector.tensor_copy(out=woven(r_il[1], 0, QUARTER), in_=planar(r_pl[1], 0, QUARTER))
        planes(1)
        for q in range(4):
            queue = nc.sync if q % 2 == 0 else nc.scalar
            queue.dma_start(out_2[0, 4 * q : 4 * q + 4, :].bitcast(I32), r_s[32 * q : 32 * q + 4, :].bitcast(I32))
